import numpy as np
import ml_dtypes


def mxq(x, axis, fmt="e4m3"):
    dtype, down = {"e4m3": (ml_dtypes.float8_e4m3fn, 7), "e5m2": (ml_dtypes.float8_e5m2, 14)}[fmt]
    v = np.moveaxis(np.asarray(x, np.float32).astype(ml_dtypes.bfloat16).astype(np.float64), axis, -1)
    blocks = v.reshape(v.shape[:-1] + (-1, 32))
    amax = np.abs(blocks).max(-1, keepdims=True)
    byte = np.maximum(np.where(amax > 0, np.frexp(amax)[1] - 1 + 127, 0) - down, 1)
    scale = np.exp2(byte - 127.0)
    codes = (blocks / scale).astype(np.float32).astype(dtype).astype(np.float64)
    return np.moveaxis((codes * scale).reshape(v.shape), -1, axis)


WIDE = False


def mx_kscale(k):
    if not WIDE:
        return np.ones(k)
    levels = np.array([10, -10, 5, -5, 0])
    if k % 512:
        return np.exp2(np.random.permutation(np.resize(levels, k // 32))).repeat(32)
    a = np.empty((k // 512, 16))
    for p in range(k // 512):
        a[p, :8] = np.random.permutation(np.resize(levels, 8))
        for g in range(8):
            far = levels[np.abs(levels - a[p, g]) >= 10]
            a[p, g + 8] = far[np.random.randint(len(far))]
    return np.exp2(a.ravel()).repeat(32)


def f64(x):
    return np.asarray(x).astype(np.float64)


def striped(idx):
    return np.tile(np.asarray(idx).reshape(-1, 16).T, (8, 1)).astype(np.uint16)


def unstriped(offs):
    return offs[:16].T.reshape(-1).astype(np.int64)


E2M1 = np.array([0.0, 0.5, 1.0, 1.5, 2.0, 3.0, 4.0, 6.0, -0.0, -0.5, -1.0, -1.5, -2.0, -3.0, -4.0, -6.0])


def pack_weight(w, fmt):
    k, n = w.shape
    w = f64(np.asarray(w, np.float32).astype(ml_dtypes.bfloat16)).reshape(k // 32, 32, n)
    amax = np.abs(w).max(1)
    if fmt == "e4m3":
        byte = np.frexp(amax)[1] - 1 + 127 - 7
    else:
        mant, ex = np.frexp(amax / 6.0)
        byte = np.where(mant > 0.5, ex, ex - 1) + 127
    byte = np.clip(np.where(amax > 0, byte, 1), 1, 254)
    scaled = (w * np.exp2(127.0 - byte)[:, None, :]).reshape(k, n).astype(np.float32)
    by_word = np.ascontiguousarray(scaled.reshape(k // 512, 128, 4, n).transpose(0, 1, 3, 2))
    if fmt == "e4m3":
        words = by_word.astype(ml_dtypes.float8_e4m3fn).view(np.uint8)
    else:
        c = by_word.astype(ml_dtypes.float4_e2m1fn).view(np.uint8) & 0xF
        words = (c[..., 0::2] | (c[..., 1::2] << 4)).reshape(k // 512, 128, 2 * n)
    return np.ascontiguousarray(words), np.ascontiguousarray(byte.astype(np.uint8).reshape(k // 512, 16, n))


def unpack_weight(words, scales, fmt):
    g, _, n = scales.shape
    words = np.ascontiguousarray(words).reshape(g, 128, n, -1)
    if fmt == "e4m3":
        vals = words.view(ml_dtypes.float8_e4m3fn).astype(np.float64)
    else:
        nib = np.empty((g, 128, n, 4), np.uint8)
        nib[..., 0::2] = words & 0xF
        nib[..., 1::2] = words >> 4
        vals = E2M1[nib]
    vals = vals * np.repeat(np.exp2(scales.astype(np.float64) - 127.0), 8, axis=1)[..., None]
    return vals.transpose(0, 1, 3, 2).reshape(g * 512, n)


def bf(x):
    return np.asarray(x, np.float32).astype(ml_dtypes.bfloat16)


def planes(Y):
    r, m = Y.shape
    b = f64(bf(Y)).reshape(r // 32, 32, m)
    amax = np.abs(b).max(1)
    byte = np.clip(np.where(amax > 0, np.frexp(amax)[1] - 1 + 127 - 7, 1), 1, 254)
    codes = (b * np.exp2(127.0 - byte)[:, None, :]).reshape(r, m).astype(np.float32).astype(ml_dtypes.float8_e4m3fn).view(np.uint8)
    words = codes.reshape(r // 512, 128, 4, m).transpose(0, 1, 3, 2)
    return np.ascontiguousarray(words), np.ascontiguousarray(byte.astype(np.uint8).reshape(r // 512, 16, m))


D, T, I, Q, E, Z, M = 512, 2048, 512, 512, 512, 1024, 1024


def setup_inputs():
    n = np.random.standard_normal
    idx = np.random.permutation(T)[:I]
    idx2 = np.random.permutation(Z)[:I]
    idx3 = np.random.permutation(M)[:I]
    fd = mx_kscale(D)
    fq = mx_kscale(Q)
    keysp = pack_weight(n((D, T)) / fd[:, None], "e2m1")
    return {
        "query": (n((D, Q)) * 1.0 / np.sqrt(D) * fd[:, None]).astype(np.float32),
        "keys_words": keysp[0],
        "keys_scales": keysp[1],
        "earl": (np.random.uniform(0.3, 1.7, (Q, Z))).astype(np.float32),
        "qs": (np.random.uniform(0.5, 2.0, (Q, 1)) * fq[:, None]).astype(np.float32),
        "msgs": (n((Q, E)) * 1 / np.sqrt(Q) / fq[:, None]).astype(np.float32),
        "old": (n((E, M)) * 1.0).astype(np.float32),
        "offs": striped(idx),
        "offs2": striped(idx2),
        "offs3": striped(idx3),
    }


def reference(query, keys_words, keys_scales, earl, qs, msgs, old, offs, offs2, offs3):
    idx = unstriped(offs)
    idx2 = unstriped(offs2)
    idx3 = unstriped(offs3)
    keysu = unpack_weight(keys_words, keys_scales, "e2m1")
    queryq = mxq(f64(query), 0, "e4m3")
    keysidxg = keysu[:, idx]
    a = queryq.T @ keysidxg
    w = a * f64(earl)[:, idx2]
    wq = w * f64(qs)
    msgsq = mxq(f64(msgs), 0, "e4m3")
    wqq = mxq(wq, 0, "e4m3")
    dl = msgsq.T @ wqq
    df = np.zeros((E, M))
    df[:, idx3] = dl
    y = f64(old) + df
    words, scales = planes(y)
    return y, words, scales

@@ -1,0 +1,217 @@
+from contextlib import ExitStack
+
+import concourse.mybir as mybir
+
+D, T, I, Q, E, Z, M = 512, 2048, 512, 512, 512, 1024, 1024
+FLOPS = 2 * D * Q * I + 2 * Q * E * I
+
+F32 = mybir.dt.float32
+BF16 = mybir.dt.bfloat16
+I32 = mybir.dt.int32
+U32 = mybir.dt.uint32
+U16 = mybir.dt.uint16
+U8 = mybir.dt.uint8
+FP8X4 = mybir.dt.float8_e4m3fn_x4
+FP4X4 = mybir.dt.float4_e2m1fn_x4
+MULT = mybir.AluOpType.mult
+ADD = mybir.AluOpType.add
+COPY = mybir.ActivationFunctionType.Copy
+
+P = 128
+PACK = 4
+LIST_COLS = I // 16
+HALF = I // 2
+
+
+def dealt_views(grouped, raw):
+    dst = grouped.rearrange("p (t m j) -> p m t j", t=PACK, j=PACK)
+    src = raw.rearrange("p j (m t) -> p m t j", t=PACK)
+    return dst, src
+
+
+def woven_views(grouped, planes):
+    dst = grouped.rearrange("p (c i t) -> p c t i", i=PACK, t=PACK)
+    src = planes.rearrange("p t (c i) -> p c t i", i=PACK)
+    return dst, src
+
+
+def tile_attend_earliertable_deliveredplanes_lean_pl_kernel(
+    tc, query, keys_words, keys_scales, earl, qs, msgs, old, offs, offs2, offs3, out_0, out_1, out_2
+):
+    nc = tc.nc
+    with ExitStack() as ctx:
+        keep = ctx.enter_context(tc.tile_pool(name="keep", bufs=1))
+        psum = ctx.enter_context(tc.psum_pool(name="psum", bufs=1))
+
+        def sbuf(name, shape, dtype):
+            return keep.tile(shape, dtype, name=name, align_bytes=64)
+
+        key_list = sbuf("key_list", [P, LIST_COLS], U16)
+        earl_list = sbuf("earl_list", [P, LIST_COLS], U16)
+        place_list = sbuf("place_list", [P, LIST_COLS], U16)
+        query_raw = sbuf("query_raw", [P, PACK, Q], F32)
+        pool_words = sbuf("pool_words", [P, T], U16)
+        pool_scales = sbuf("pool_scales", [P, T], U8)
+        earl_rows = [sbuf("earl_rows%d" % r, [P, Z], F32) for r in range(PACK)]
+        row_factor = sbuf("row_factor", [P, PACK], F32)
+        msgs_raw = [sbuf("msgs_raw%d" % h, [P, PACK, E // 2], F32) for h in range(2)]
+        old_rows = sbuf("old_rows", [P, PACK, M], F32)
+        placed = [sbuf("placed%d" % j, [P, M], F32) for j in range(PACK)]
+
+        nc.gpsimd.memset(pool_scales[:].bitcast(I32), 0)
+        for j in range(PACK):
+            nc.gpsimd.memset(placed[j][:], 0.0)
+
+        nc.sync.dma_start(out=pool_words[:].bitcast(I32), in_=keys_words[0].bitcast(I32))
+        nc.sync.dma_start(key_list[:], offs)
+        nc.sync.dma_start(out=query_raw[:], in_=query.rearrange("(p j) q -> p j q", j=PACK))
+        for quad in range(4):
+            nc.scalar.dma_start(
+                out=pool_scales[32 * quad : 32 * quad + 4, :].bitcast(I32),
+                in_=keys_scales[0, 4 * quad : 4 * quad + 4, :].bitcast(I32),
+            )
+        nc.sync.dma_start(earl_list[:], offs2)
+        earl_by_place = earl.rearrange("(p r) z -> p r z", r=PACK)
+        nc.sync.dma_start(out=earl_rows[0][:], in_=earl_by_place[:, 0, :])
+        nc.sync.dma_start(out=row_factor[:], in_=qs.rearrange("(p r) o -> p (r o)", r=PACK))
+        for r in range(1, PACK):
+            nc.sync.dma_start(out=earl_rows[r][:], in_=earl_by_place[:, r, :])
+        msgs_by_place = msgs.rearrange("(p j) e -> p j e", j=PACK)
+        for h in range(2):
+            nc.sync.dma_start(out=msgs_raw[h][:], in_=msgs_by_place[:, :, h * (E // 2) : (h + 1) * (E // 2)])
+        nc.sync.dma_start(place_list[:], offs3)
+        nc.sync.dma_start(out=old_rows[:], in_=old.rearrange("(p j) m -> p j m", j=PACK))
+
+        query_grouped = sbuf("query_grouped", [P, PACK * Q], BF16)
+        query_codes = sbuf("query_codes", [P, Q], U32)
+        query_scales = sbuf("query_scales", [P, Q], U8)
+        key_words = sbuf("key_words", [P, I], U16)
+        key_scales = sbuf("key_scales", [P, I], U8)
+        nc.vector.tensor_copy(key_words[:], pool_words[:].indirect(key_list[:]))
+        nc.vector.tensor_copy(key_scales[:], pool_scales[:].indirect(key_list[:]))
+        dst, src = dealt_views(query_grouped[:], query_raw[:])
+        nc.scalar.copy(out=dst[:, :44], in_=src[:, :44])
+        nc.vector.tensor_copy(out=dst[:, 44:], in_=src[:, 44:])
+        nc.vector.quantize_mx(out=query_codes[:].bitcast(FP8X4), scales=query_scales[:], in_=query_grouped[:])
+
+        weights = sbuf("weights", [P, PACK, I], BF16)
+        earl_listed = [sbuf("earl_listed%d" % r, [P, I], F32) for r in range(PACK)]
+        nc.scalar.activation(earl_listed[0][:], earl_rows[0][:].indirect(earl_list[:]), COPY)
+        nc.vector.tensor_copy(earl_listed[1][:], earl_rows[1][:].indirect(earl_list[:]))
+        nc.scalar.activation(earl_listed[2][:], earl_rows[2][:].indirect(earl_list[:]), COPY)
+        for r in range(PACK):
+            cols = slice(r * P, (r + 1) * P)
+            scores = psum.tile([P, I], F32, name="scores%d" % r)
+            nc.tensor.matmul_mx(
+                out=scores[:],
+                lhsT=query_codes[:, cols].bitcast(FP8X4),
+                lhsT_scale=query_scales[:, cols],
+                rhs=key_words[:].bitcast(FP4X4),
+                rhs_scale=key_scales[:],
+                start=True,
+                stop=True,
+            )
+            if r == 2:
+                nc.vector.tensor_copy(earl_listed[3][:, :HALF], earl_rows[3][:].indirect(earl_list[:, : LIST_COLS // 2]))
+                nc.scalar.activation(earl_listed[3][:, HALF:], earl_rows[3][:].indirect(earl_list[:, LIST_COLS // 2 :]), COPY)
+            nc.vector.scalar_tensor_tensor(
+                out=weights[:, r, :], in0=scores[:], scalar=row_factor[:, r : r + 1], in1=earl_listed[r][:], op0=MULT, op1=MULT
+            )
+
+        weights_grouped = sbuf("weights_grouped", [P, PACK * I], BF16)
+        weights_codes = sbuf("weights_codes", [P, I], U32)
+        weights_scales = sbuf("weights_scales", [P, I], U8)
+        dst, src = woven_views(weights_grouped[:], weights[:])
+        nc.vector.tensor_copy(out=dst, in_=src)
+
+        msgs_grouped = sbuf("msgs_grouped", [P, PACK * E], BF16)
+        msgs_codes = sbuf("msgs_codes", [P, E], U32)
+        msgs_scales = sbuf("msgs_scales", [P, E], U8)
+        for h in range(2):
+            dst, src = dealt_views(msgs_grouped[:], msgs_raw[h][:])
+            nc.scalar.copy(out=dst[:, h * (P // 2) : (h + 1) * (P // 2)], in_=src)
+        nc.vector.quantize_mx(out=weights_codes[:].bitcast(FP8X4), scales=weights_scales[:], in_=weights_grouped[:])
+        for h in range(2):
+            cols = slice(h * (E // 2), (h + 1) * (E // 2))
+            nc.vector.quantize_mx(
+                out=msgs_codes[:, cols].bitcast(FP8X4),
+                scales=msgs_scales[:, cols],
+                in_=msgs_grouped[:, h * 2 * E : (h + 1) * 2 * E],
+            )
+
+        sums = []
+        for j in range(PACK):
+            cols = slice(j * P, (j + 1) * P)
+            bank = psum.tile([P, I], F32, name="sums%d" % j)
+            nc.tensor.matmul_mx(
+                out=bank[:],
+                lhsT=msgs_codes[:, cols].bitcast(FP8X4),
+                lhsT_scale=msgs_scales[:, cols],
+                rhs=weights_codes[:].bitcast(FP8X4),
+                rhs_scale=weights_scales[:],
+                start=True,
+                stop=True,
+            )
+            delivered = sbuf("delivered%d" % j, [P, I], F32)
+            if j == 0:
+                nc.vector.tensor_copy(out=delivered[:], in_=bank[:])
+            else:
+                nc.scalar.copy(out=delivered[:], in_=bank[:])
+            sums.append(delivered)
+
+        result = sbuf("result", [P, PACK, M], F32)
+        out_by_place = out_0.rearrange("(p j) m -> p j m", j=PACK)
+
+        def scatter(engine_is_vector, j, first, last):
+            window = placed[j][:].indirect(place_list[:, first // 16 : last // 16])
+            if engine_is_vector:
+                nc.vector.tensor_copy(window, sums[j][:, first:last])
+            else:
+                nc.scalar.activation(window, sums[j][:, first:last], COPY)
+
+        def add_old(j, first, last):
+            nc.vector.tensor_tensor(
+                out=result[:, j, first:last], in0=old_rows[:, j, first:last], in1=placed[j][:, first:last], op=ADD
+            )
+
+        def store(j):
+            nc.sync.dma_start(out=out_by_place[:, j, :], in_=result[:, j, :])
+
+        scatter(True, 0, 0, I)
+        scatter(False, 1, 0, HALF)
+        scatter(False, 1, HALF, I)
+        add_old(0, 0, M)
+        store(0)
+        scatter(True, 2, 0, 384)
+        scatter(False, 3, 0, HALF)
+        scatter(False, 3, HALF, I)
+        add_old(1, 0, M)
+        store(1)
+        scatter(False, 2, 384, I)
+        add_old(3, 0, M)
+        store(3)
+        add_old(2, 0, M // 2)
+        add_old(2, M // 2, M)
+        store(2)
+
+        result_grouped = sbuf("result_grouped", [P, PACK * M], BF16)
+        result_codes = sbuf("result_codes", [P, M], U32)
+        result_scales = sbuf("result_scales", [P, M], U8)
+        dst, src = woven_views(result_grouped[:], result[:])
+        out_words = out_1[0].rearrange("p c r -> p (c r)").bitcast(I32)
+        nc.scalar.copy(out=dst[:, 0:128], in_=src[:, 0:128])
+        nc.vector.tensor_copy(out=dst[:, 128:256], in_=src[:, 128:256])
+        for h in (1, 0):
+            cols = slice(h * 512, (h + 1) * 512)
+            nc.vector.quantize_mx(
+                out=result_codes[:, cols].bitcast(FP8X4),
+                scales=result_scales[:, cols],
+                in_=result_grouped[:, h * 2048 : (h + 1) * 2048],
+            )
+            nc.sync.dma_start(out=out_words[:, cols], in_=result_codes[:, cols].bitcast(I32))
+        for quad in range(4):
+            queue = nc.sync if quad % 2 == 0 else nc.scalar
+            queue.dma_start(
+                out=out_2[0, 4 * quad : 4 * quad + 4, :].bitcast(I32),
+                in_=result_scales[32 * quad : 32 * quad + 4, :].bitcast(I32),
+            )

@@ -24,8 +24,8 @@ HALF = I // 2
 
 
 def dealt_views(grouped, raw):
-    dst = grouped.rearrange("p (t m j) -> p m t j", t=PACK, j=PACK)
-    src = raw.rearrange("p j (m t) -> p m t j", t=PACK)
+    dst = grouped.rearrange("p (t m j) -> p m j t", t=PACK, j=PACK)
+    src = raw.rearrange("p j (m t) -> p m j t", t=PACK)
     return dst, src
 
 
@@ -43,8 +43,8 @@ def tile_attend_earliertable_deliveredplanes_lean_pl_kernel(
         keep = ctx.enter_context(tc.tile_pool(name="keep", bufs=1))
         psum = ctx.enter_context(tc.psum_pool(name="psum", bufs=1))
 
-        def sbuf(name, shape, dtype):
-            return keep.tile(shape, dtype, name=name, align_bytes=64)
+        def sbuf(name, shape, dtype, tag=None):
+            return keep.tile(shape, dtype, name=name, tag=tag or name, align_bytes=64)
 
         key_list = sbuf("key_list", [P, LIST_COLS], U16)
         earl_list = sbuf("earl_list", [P, LIST_COLS], U16)
@@ -55,47 +55,56 @@ def tile_attend_earliertable_deliveredplanes_lean_pl_kernel(
         earl_rows = [sbuf("earl_rows%d" % r, [P, Z], F32) for r in range(PACK)]
         row_factor = sbuf("row_factor", [P, PACK], F32)
         msgs_raw = [sbuf("msgs_raw%d" % h, [P, PACK, E // 2], F32) for h in range(2)]
-        old_rows = sbuf("old_rows", [P, PACK, M], F32)
+        old_rows = [sbuf("old_rows%d" % h, [P, 2, M], F32) for h in range(2)]
         placed = [sbuf("placed%d" % j, [P, M], F32) for j in range(PACK)]
 
-        nc.gpsimd.memset(pool_scales[:].bitcast(I32), 0)
+        nc.vector.memset(pool_scales[:].bitcast(I32), 0)
+        nc.gpsimd.dma_start(out=row_factor[:], in_=qs.rearrange("(p r) o -> p (r o)", r=PACK))
         for j in range(PACK):
-            nc.gpsimd.memset(placed[j][:], 0.0)
+            (nc.vector if j < 2 else nc.gpsimd).memset(placed[j][:], 0.0)
 
+        earl_by_place = earl.rearrange("(p r) z -> p r z", r=PACK)
         nc.sync.dma_start(out=pool_words[:].bitcast(I32), in_=keys_words[0].bitcast(I32))
         nc.sync.dma_start(key_list[:], offs)
+        nc.sync.dma_start(earl_list[:], offs2)
         nc.sync.dma_start(out=query_raw[:], in_=query.rearrange("(p j) q -> p j q", j=PACK))
         for quad in range(4):
             nc.scalar.dma_start(
                 out=pool_scales[32 * quad : 32 * quad + 4, :].bitcast(I32),
                 in_=keys_scales[0, 4 * quad : 4 * quad + 4, :].bitcast(I32),
             )
-        nc.sync.dma_start(earl_list[:], offs2)
-        earl_by_place = earl.rearrange("(p r) z -> p r z", r=PACK)
-        nc.sync.dma_start(out=earl_rows[0][:], in_=earl_by_place[:, 0, :])
-        nc.sync.dma_start(out=row_factor[:], in_=qs.rearrange("(p r) o -> p (r o)", r=PACK))
-        for r in range(1, PACK):
+        for r in range(PACK):
             nc.sync.dma_start(out=earl_rows[r][:], in_=earl_by_place[:, r, :])
         msgs_by_place = msgs.rearrange("(p j) e -> p j e", j=PACK)
         for h in range(2):
             nc.sync.dma_start(out=msgs_raw[h][:], in_=msgs_by_place[:, :, h * (E // 2) : (h + 1) * (E // 2)])
         nc.sync.dma_start(place_list[:], offs3)
-        nc.sync.dma_start(out=old_rows[:], in_=old.rearrange("(p j) m -> p j m", j=PACK))
+        old_by_place = old.rearrange("(p j) m -> p j m", j=PACK)
+        for h in range(2):
+            nc.sync.dma_start(out=old_rows[h][:], in_=old_by_place[:, 2 * h : 2 * h + 2, :])
 
-        query_grouped = sbuf("query_grouped", [P, PACK * Q], BF16)
+        query_grouped = [
+            sbuf("query_grouped0", [P, 2 * Q], BF16),
+            sbuf("query_grouped1", [P, 2 * Q], BF16, tag="relay"),
+        ]
         query_codes = sbuf("query_codes", [P, Q], U32)
         query_scales = sbuf("query_scales", [P, Q], U8)
         key_words = sbuf("key_words", [P, I], U16)
         key_scales = sbuf("key_scales", [P, I], U8)
         nc.vector.tensor_copy(key_words[:], pool_words[:].indirect(key_list[:]))
         nc.vector.tensor_copy(key_scales[:], pool_scales[:].indirect(key_list[:]))
-        dst, src = dealt_views(query_grouped[:], query_raw[:])
-        nc.scalar.copy(out=dst[:, :44], in_=src[:, :44])
-        nc.vector.tensor_copy(out=dst[:, 44:], in_=src[:, 44:])
-        nc.vector.quantize_mx(out=query_codes[:].bitcast(FP8X4), scales=query_scales[:], in_=query_grouped[:])
+        src = query_raw[:].rearrange("p j (m t) -> p m j t", t=PACK)
+        for h, copy in enumerate((nc.vector.tensor_copy, nc.scalar.copy)):
+            dst = query_grouped[h][:].rearrange("p (t m j) -> p m j t", t=2, j=PACK)
+            copy(out=dst, in_=src[:, :, :, 2 * h : 2 * h + 2])
+        for h in range(2):
+            cols = slice(h * (Q // 2), (h + 1) * (Q // 2))
+            nc.vector.quantize_mx(
+                out=query_codes[:, cols].bitcast(FP8X4), scales=query_scales[:, cols], in_=query_grouped[h][:]
+            )
 
         weights = sbuf("weights", [P, PACK, I], BF16)
-        earl_listed = [sbuf("earl_listed%d" % r, [P, I], F32) for r in range(PACK)]
+        earl_listed = [sbuf("earl_listed%d" % r, [P, I], F32, tag="relay" if r == 1 else None) for r in range(PACK - 1)]
         nc.scalar.activation(earl_listed[0][:], earl_rows[0][:].indirect(earl_list[:]), COPY)
         nc.vector.tensor_copy(earl_listed[1][:], earl_rows[1][:].indirect(earl_list[:]))
         nc.scalar.activation(earl_listed[2][:], earl_rows[2][:].indirect(earl_list[:]), COPY)
@@ -112,17 +121,25 @@ def tile_attend_earliertable_deliveredplanes_lean_pl_kernel(
                 stop=True,
             )
             if r == 2:
+                earl_listed.append(sbuf("earl_listed3", [P, I], F32, tag="relay"))
                 nc.vector.tensor_copy(earl_listed[3][:, :HALF], earl_rows[3][:].indirect(earl_list[:, : LIST_COLS // 2]))
                 nc.scalar.activation(earl_listed[3][:, HALF:], earl_rows[3][:].indirect(earl_list[:, LIST_COLS // 2 :]), COPY)
-            nc.vector.scalar_tensor_tensor(
-                out=weights[:, r, :], in0=scores[:], scalar=row_factor[:, r : r + 1], in1=earl_listed[r][:], op0=MULT, op1=MULT
-            )
+            for first, last in ((0, I),) if r < PACK - 1 else ((0, HALF), (HALF, I)):
+                nc.vector.scalar_tensor_tensor(
+                    out=weights[:, r, first:last],
+                    in0=scores[:, first:last],
+                    scalar=row_factor[:, r : r + 1],
+                    in1=earl_listed[r][:, first:last],
+                    op0=MULT,
+                    op1=MULT,
+                )
 
         weights_grouped = sbuf("weights_grouped", [P, PACK * I], BF16)
         weights_codes = sbuf("weights_codes", [P, I], U32)
         weights_scales = sbuf("weights_scales", [P, I], U8)
         dst, src = woven_views(weights_grouped[:], weights[:])
-        nc.vector.tensor_copy(out=dst, in_=src)
+        for h in range(2):
+            nc.vector.tensor_copy(out=dst[:, h * 64 : (h + 1) * 64], in_=src[:, h * 64 : (h + 1) * 64])
 
         msgs_grouped = sbuf("msgs_grouped", [P, PACK * E], BF16)
         msgs_codes = sbuf("msgs_codes", [P, E], U32)
@@ -130,7 +147,13 @@ def tile_attend_earliertable_deliveredplanes_lean_pl_kernel(
         for h in range(2):
             dst, src = dealt_views(msgs_grouped[:], msgs_raw[h][:])
             nc.scalar.copy(out=dst[:, h * (P // 2) : (h + 1) * (P // 2)], in_=src)
-        nc.vector.quantize_mx(out=weights_codes[:].bitcast(FP8X4), scales=weights_scales[:], in_=weights_grouped[:])
+        for h in range(2):
+            cols = slice(h * HALF, (h + 1) * HALF)
+            nc.vector.quantize_mx(
+                out=weights_codes[:, cols].bitcast(FP8X4),
+                scales=weights_scales[:, cols],
+                in_=weights_grouped[:, h * PACK * HALF : (h + 1) * PACK * HALF],
+            )
         for h in range(2):
             cols = slice(h * (E // 2), (h + 1) * (E // 2))
             nc.vector.quantize_mx(
@@ -139,27 +162,24 @@ def tile_attend_earliertable_deliveredplanes_lean_pl_kernel(
                 in_=msgs_grouped[:, h * 2 * E : (h + 1) * 2 * E],
             )
 
-        sums = []
-        for j in range(PACK):
+        def deliver(j, first, last, tag):
             cols = slice(j * P, (j + 1) * P)
-            bank = psum.tile([P, I], F32, name="sums%d" % j)
+            bank = psum.tile([P, last - first], F32, name="sums%d_%d" % (j, first), tag=tag)
             nc.tensor.matmul_mx(
                 out=bank[:],
                 lhsT=msgs_codes[:, cols].bitcast(FP8X4),
                 lhsT_scale=msgs_scales[:, cols],
-                rhs=weights_codes[:].bitcast(FP8X4),
-                rhs_scale=weights_scales[:],
+                rhs=weights_codes[:, first:last].bitcast(FP8X4),
+                rhs_scale=weights_scales[:, first:last],
                 start=True,
                 stop=True,
             )
-            delivered = sbuf("delivered%d" % j, [P, I], F32)
-            if j == 0:
-                nc.vector.tensor_copy(out=delivered[:], in_=bank[:])
-            else:
-                nc.scalar.copy(out=delivered[:], in_=bank[:])
-            sums.append(delivered)
+            return bank
 
-        result = sbuf("result", [P, PACK, M], F32)
+        bank0 = [deliver(0, 0, HALF, "sums0"), deliver(0, HALF, I, "scores0")]
+        banks = {j: deliver(j, 0, I, "sums%d" % j) for j in (2, 1, 3)}
+
+        sums = [sbuf("sums_sb%d" % j, [P, I], F32, tag="relay_out" if j == 2 else None) for j in range(PACK)]
         out_by_place = out_0.rearrange("(p j) m -> p j m", j=PACK)
 
         def scatter(engine_is_vector, j, first, last):
@@ -169,48 +189,51 @@ def tile_attend_earliertable_deliveredplanes_lean_pl_kernel(
             else:
                 nc.scalar.activation(window, sums[j][:, first:last], COPY)
 
-        def add_old(j, first, last):
-            nc.vector.tensor_tensor(
-                out=result[:, j, first:last], in0=old_rows[:, j, first:last], in1=placed[j][:, first:last], op=ADD
+        def add_old(j, first, last, engine=nc.vector):
+            engine.tensor_tensor(
+                out=result[:, j, first:last], in0=old_rows[j // 2][:, j % 2, first:last], in1=placed[j][:, first:last], op=ADD
             )
 
         def store(j):
             nc.sync.dma_start(out=out_by_place[:, j, :], in_=result[:, j, :])
 
-        scatter(True, 0, 0, I)
-        scatter(False, 1, 0, HALF)
-        scatter(False, 1, HALF, I)
-        add_old(0, 0, M)
-        store(0)
-        scatter(True, 2, 0, 384)
-        scatter(False, 3, 0, HALF)
-        scatter(False, 3, HALF, I)
-        add_old(1, 0, M)
-        store(1)
+        for h in range(2):
+            nc.vector.tensor_copy(out=sums[0][:, h * HALF : (h + 1) * HALF], in_=bank0[h][:])
+        for h in range(2):
+            scatter(True, 0, h * HALF, (h + 1) * HALF)
+        nc.scalar.copy(out=sums[2][:], in_=banks[2][:])
+        nc.scalar.copy(out=sums[1][:], in_=banks[1][:])
         scatter(False, 2, 384, I)
-        add_old(3, 0, M)
+        nc.scalar.copy(out=sums[3][:], in_=banks[3][:])
+        scatter(True, 2, 0, 384)
+        for j in (1, 3):
+            scatter(False, j, 0, HALF)
+            scatter(False, j, HALF, I)
+        result = sbuf("result", [P, PACK, M], F32, tag="relay_out")
+        for j in (0, 1, 2):
+            add_old(j, 0, M)
+            store(j)
+        pieces = ((0, 256), (256, 512), (512, M))
+        for first, last in (pieces[0], pieces[2], pieces[1]):
+            add_old(3, first, last)
         store(3)
-        add_old(2, 0, M // 2)
-        add_old(2, M // 2, M)
-        store(2)
 
         result_grouped = sbuf("result_grouped", [P, PACK * M], BF16)
         result_codes = sbuf("result_codes", [P, M], U32)
         result_scales = sbuf("result_scales", [P, M], U8)
         dst, src = woven_views(result_grouped[:], result[:])
         out_words = out_1[0].rearrange("p c r -> p (c r)").bitcast(I32)
-        nc.scalar.copy(out=dst[:, 0:128], in_=src[:, 0:128])
-        nc.vector.tensor_copy(out=dst[:, 128:256], in_=src[:, 128:256])
-        for h in (1, 0):
-            cols = slice(h * 512, (h + 1) * 512)
+        for (first, last), copy in zip(pieces, (nc.scalar.copy, nc.scalar.copy, nc.vector.tensor_copy)):
+            copy(out=dst[:, first // PACK : last // PACK], in_=src[:, first // PACK : last // PACK])
+        for first, last in (pieces[0], pieces[2], pieces[1]):
             nc.vector.quantize_mx(
-                out=result_codes[:, cols].bitcast(FP8X4),
-                scales=result_scales[:, cols],
-                in_=result_grouped[:, h * 2048 : (h + 1) * 2048],
+                out=result_codes[:, first:last].bitcast(FP8X4),
+                scales=result_scales[:, first:last],
+                in_=result_grouped[:, first * PACK : last * PACK],
             )
-            nc.sync.dma_start(out=out_words[:, cols], in_=result_codes[:, cols].bitcast(I32))
+            nc.sync.dma_start(out=out_words[:, first:last], in_=result_codes[:, first:last].bitcast(I32))
         for quad in range(4):
-            queue = nc.sync if quad % 2 == 0 else nc.scalar
+            queue = nc.scalar if quad % 2 == 0 else nc.sync
             queue.dma_start(
                 out=out_2[0, 4 * quad : 4 * quad + 4, :].bitcast(I32),
                 in_=result_scales[32 * quad : 32 * quad + 4, :].bitcast(I32),

@@ -21,6 +21,8 @@ P = 128
 PACK = 4
 LIST_COLS = I // 16
 HALF = I // 2
+SCALAR_DEALS = 24
+SCALAR_PLACES = 192
 
 
 def dealt_views(grouped, raw):
@@ -58,7 +60,7 @@ def tile_attend_earliertable_deliveredplanes_lean_pl_kernel(
         old_rows = [sbuf("old_rows%d" % h, [P, 2, M], F32) for h in range(2)]
         placed = [sbuf("placed%d" % j, [P, M], F32) for j in range(PACK)]
 
-        nc.vector.memset(pool_scales[:].bitcast(I32), 0)
+        nc.gpsimd.memset(pool_scales[:].bitcast(I32), 0)
         nc.gpsimd.dma_start(out=row_factor[:], in_=qs.rearrange("(p r) o -> p (r o)", r=PACK))
         for j in range(PACK):
             (nc.vector if j < 2 else nc.gpsimd).memset(placed[j][:], 0.0)
@@ -66,15 +68,16 @@ def tile_attend_earliertable_deliveredplanes_lean_pl_kernel(
         earl_by_place = earl.rearrange("(p r) z -> p r z", r=PACK)
         nc.sync.dma_start(out=pool_words[:].bitcast(I32), in_=keys_words[0].bitcast(I32))
         nc.sync.dma_start(key_list[:], offs)
-        nc.sync.dma_start(earl_list[:], offs2)
-        nc.sync.dma_start(out=query_raw[:], in_=query.rearrange("(p j) q -> p j q", j=PACK))
         for quad in range(4):
-            nc.scalar.dma_start(
+            nc.sync.dma_start(
                 out=pool_scales[32 * quad : 32 * quad + 4, :].bitcast(I32),
                 in_=keys_scales[0, 4 * quad : 4 * quad + 4, :].bitcast(I32),
             )
+        nc.sync.dma_start(out=query_raw[:], in_=query.rearrange("(p j) q -> p j q", j=PACK))
         for r in range(PACK):
             nc.sync.dma_start(out=earl_rows[r][:], in_=earl_by_place[:, r, :])
+            if r == 0:
+                nc.sync.dma_start(earl_list[:], offs2)
         msgs_by_place = msgs.rearrange("(p j) e -> p j e", j=PACK)
         for h in range(2):
             nc.sync.dma_start(out=msgs_raw[h][:], in_=msgs_by_place[:, :, h * (E // 2) : (h + 1) * (E // 2)])
@@ -103,11 +106,14 @@ def tile_attend_earliertable_deliveredplanes_lean_pl_kernel(
                 out=query_codes[:, cols].bitcast(FP8X4), scales=query_scales[:, cols], in_=query_grouped[h][:]
             )
 
-        weights = sbuf("weights", [P, PACK, I], BF16)
-        earl_listed = [sbuf("earl_listed%d" % r, [P, I], F32, tag="relay" if r == 1 else None) for r in range(PACK - 1)]
-        nc.scalar.activation(earl_listed[0][:], earl_rows[0][:].indirect(earl_list[:]), COPY)
-        nc.vector.tensor_copy(earl_listed[1][:], earl_rows[1][:].indirect(earl_list[:]))
+        weights = sbuf("weights", [P, 2, PACK, HALF], BF16)
+        earl_listed = [sbuf("earl_listed%d" % r, [P, I], F32, tag="relay" if r == 0 else None) for r in range(PACK)]
+        nc.vector.tensor_copy(earl_listed[0][:], earl_rows[0][:].indirect(earl_list[:]))
+        nc.scalar.activation(earl_listed[1][:], earl_rows[1][:].indirect(earl_list[:]), COPY)
         nc.scalar.activation(earl_listed[2][:], earl_rows[2][:].indirect(earl_list[:]), COPY)
+        for h in range(2):
+            half_list = earl_list[:, h * (LIST_COLS // 2) : (h + 1) * (LIST_COLS // 2)]
+            nc.scalar.activation(earl_listed[3][:, h * HALF : (h + 1) * HALF], earl_rows[3][:].indirect(half_list), COPY)
         for r in range(PACK):
             cols = slice(r * P, (r + 1) * P)
             scores = psum.tile([P, I], F32, name="scores%d" % r)
@@ -120,96 +126,90 @@ def tile_attend_earliertable_deliveredplanes_lean_pl_kernel(
                 start=True,
                 stop=True,
             )
-            if r == 2:
-                earl_listed.append(sbuf("earl_listed3", [P, I], F32, tag="relay"))
-                nc.vector.tensor_copy(earl_listed[3][:, :HALF], earl_rows[3][:].indirect(earl_list[:, : LIST_COLS // 2]))
-                nc.scalar.activation(earl_listed[3][:, HALF:], earl_rows[3][:].indirect(earl_list[:, LIST_COLS // 2 :]), COPY)
-            for first, last in ((0, I),) if r < PACK - 1 else ((0, HALF), (HALF, I)):
+            for halves in (slice(0, 2),) if r < PACK - 1 else (slice(0, 1), slice(1, 2)):
                 nc.vector.scalar_tensor_tensor(
-                    out=weights[:, r, first:last],
-                    in0=scores[:, first:last],
+                    out=weights[:, halves, r, :],
+                    in0=scores[:].rearrange("p (h i) -> p h i", h=2)[:, halves],
                     scalar=row_factor[:, r : r + 1],
-                    in1=earl_listed[r][:, first:last],
+                    in1=earl_listed[r][:].rearrange("p (h i) -> p h i", h=2)[:, halves],
                     op0=MULT,
                     op1=MULT,
                 )
 
-        weights_grouped = sbuf("weights_grouped", [P, PACK * I], BF16)
-        weights_codes = sbuf("weights_codes", [P, I], U32)
-        weights_scales = sbuf("weights_scales", [P, I], U8)
-        dst, src = woven_views(weights_grouped[:], weights[:])
-        for h in range(2):
-            nc.vector.tensor_copy(out=dst[:, h * 64 : (h + 1) * 64], in_=src[:, h * 64 : (h + 1) * 64])
+        grouped = sbuf("grouped", [P, PACK * (HALF + E)], BF16)
+        codes = sbuf("codes", [P, HALF + E // 2], U32)
+        scales = sbuf("scales", [P, HALF + E // 2], U8)
+        late_msgs_codes = sbuf("late_msgs_codes", [P, E // 2], U32)
+        late_msgs_scales = sbuf("late_msgs_scales", [P, E // 2], U8)
+        late_grouped = sbuf("late_grouped", [P, PACK * HALF], BF16, tag="msgs_raw1")
+        late_codes = sbuf("late_codes", [P, HALF], U32)
+        late_scales = sbuf("late_scales", [P, HALF], U8)
 
-        msgs_grouped = sbuf("msgs_grouped", [P, PACK * E], BF16)
-        msgs_codes = sbuf("msgs_codes", [P, E], U32)
-        msgs_scales = sbuf("msgs_scales", [P, E], U8)
-        for h in range(2):
-            dst, src = dealt_views(msgs_grouped[:], msgs_raw[h][:])
-            nc.scalar.copy(out=dst[:, h * (P // 2) : (h + 1) * (P // 2)], in_=src)
-        for h in range(2):
-            cols = slice(h * HALF, (h + 1) * HALF)
-            nc.vector.quantize_mx(
-                out=weights_codes[:, cols].bitcast(FP8X4),
-                scales=weights_scales[:, cols],
-                in_=weights_grouped[:, h * PACK * HALF : (h + 1) * PACK * HALF],
-            )
-        for h in range(2):
-            cols = slice(h * (E // 2), (h + 1) * (E // 2))
-            nc.vector.quantize_mx(
-                out=msgs_codes[:, cols].bitcast(FP8X4),
-                scales=msgs_scales[:, cols],
-                in_=msgs_grouped[:, h * 2 * E : (h + 1) * 2 * E],
-            )
+        def deal_msgs(copy, h, first, last):
+            dst, src = dealt_views(grouped[:, PACK * HALF :], msgs_raw[h][:])
+            copy(out=dst[:, h * (P // 2) + first : h * (P // 2) + last], in_=src[:, first:last])
 
-        def deliver(j, first, last, tag):
-            cols = slice(j * P, (j + 1) * P)
-            bank = psum.tile([P, last - first], F32, name="sums%d_%d" % (j, first), tag=tag)
-            nc.tensor.matmul_mx(
-                out=bank[:],
-                lhsT=msgs_codes[:, cols].bitcast(FP8X4),
-                lhsT_scale=msgs_scales[:, cols],
-                rhs=weights_codes[:, first:last].bitcast(FP8X4),
-                rhs_scale=weights_scales[:, first:last],
-                start=True,
-                stop=True,
-            )
-            return bank
+        deal_msgs(nc.scalar.copy, 0, 0, P // 2)
+        deal_msgs(nc.scalar.copy, 1, 0, SCALAR_DEALS)
+        dst, src = woven_views(grouped[:, : PACK * HALF], weights[:, 0])
+        nc.vector.tensor_copy(out=dst, in_=src)
+        deal_msgs(nc.vector.tensor_copy, 1, SCALAR_DEALS, P // 2)
+        split = PACK * (HALF + E // 2)
+        nc.vector.quantize_mx(out=codes[:].bitcast(FP8X4), scales=scales[:], in_=grouped[:, :split])
+        nc.vector.quantize_mx(out=late_msgs_codes[:].bitcast(FP8X4), scales=late_msgs_scales[:], in_=grouped[:, split:])
+        dst, src = woven_views(late_grouped[:], weights[:, 1])
+        nc.scalar.copy(out=dst, in_=src)
+        nc.vector.quantize_mx(out=late_codes[:].bitcast(FP8X4), scales=late_scales[:], in_=late_grouped[:])
 
-        bank0 = [deliver(0, 0, HALF, "sums0"), deliver(0, HALF, I, "scores0")]
-        banks = {j: deliver(j, 0, I, "sums%d" % j) for j in (2, 1, 3)}
+        msgs_operand = [
+            (codes[:, HALF + j * P : HALF + (j + 1) * P], scales[:, HALF + j * P : HALF + (j + 1) * P]) for j in range(2)
+        ] + [(late_msgs_codes[:, j * P : (j + 1) * P], late_msgs_scales[:, j * P : (j + 1) * P]) for j in range(2)]
+        weights_operand = [(codes[:, :HALF], scales[:, :HALF]), (late_codes[:], late_scales[:])]
+        banks = {}
+        for h in range(2):
+            for j in (1, 0, 2, 3) if h == 0 else range(PACK):
+                tag = "sums%d" % j if h == 0 else "scores%d" % j
+                banks[j, h] = psum.tile([P, HALF], F32, name="sums%d_%d" % (j, h), tag=tag)
+                nc.tensor.matmul_mx(
+                    out=banks[j, h][:],
+                    lhsT=msgs_operand[j][0].bitcast(FP8X4),
+                    lhsT_scale=msgs_operand[j][1],
+                    rhs=weights_operand[h][0].bitcast(FP8X4),
+                    rhs_scale=weights_operand[h][1],
+                    start=True,
+                    stop=True,
+                )
 
-        sums = [sbuf("sums_sb%d" % j, [P, I], F32, tag="relay_out" if j == 2 else None) for j in range(PACK)]
         out_by_place = out_0.rearrange("(p j) m -> p j m", j=PACK)
+        result = sbuf("result", [P, PACK, M], F32)
 
-        def scatter(engine_is_vector, j, first, last):
+        sums = [sbuf("sums_sb%d" % j, [P, I], F32) for j in range(PACK)]
+
+        def place(on_vector, j, h, first, last):
+            out_of_bank = sums[j][:, h * HALF : (h + 1) * HALF]
             window = placed[j][:].indirect(place_list[:, first // 16 : last // 16])
-            if engine_is_vector:
+            if on_vector:
+                nc.vector.tensor_copy(out=out_of_bank, in_=banks[j, h][:])
                 nc.vector.tensor_copy(window, sums[j][:, first:last])
             else:
+                nc.scalar.copy(out=out_of_bank, in_=banks[j, h][:])
                 nc.scalar.activation(window, sums[j][:, first:last], COPY)
 
-        def add_old(j, first, last, engine=nc.vector):
-            engine.tensor_tensor(
+        def add_old(j, first, last):
+            nc.vector.tensor_tensor(
                 out=result[:, j, first:last], in0=old_rows[j // 2][:, j % 2, first:last], in1=placed[j][:, first:last], op=ADD
             )
 
         def store(j):
             nc.sync.dma_start(out=out_by_place[:, j, :], in_=result[:, j, :])
 
+        place(False, 1, 0, 0, SCALAR_PLACES)
+        for j in (2, 3):
+            for h in range(2):
+                place(False, j, h, h * HALF, (h + 1) * HALF)
         for h in range(2):
-            nc.vector.tensor_copy(out=sums[0][:, h * HALF : (h + 1) * HALF], in_=bank0[h][:])
-        for h in range(2):
-            scatter(True, 0, h * HALF, (h + 1) * HALF)
-        nc.scalar.copy(out=sums[2][:], in_=banks[2][:])
-        nc.scalar.copy(out=sums[1][:], in_=banks[1][:])
-        scatter(False, 2, 384, I)
-        nc.scalar.copy(out=sums[3][:], in_=banks[3][:])
-        scatter(True, 2, 0, 384)
-        for j in (1, 3):
-            scatter(False, j, 0, HALF)
-            scatter(False, j, HALF, I)
-        result = sbuf("result", [P, PACK, M], F32, tag="relay_out")
+            place(True, 0, h, h * HALF, (h + 1) * HALF)
+        place(True, 1, 1, SCALAR_PLACES, I)
         for j in (0, 1, 2):
             add_old(j, 0, M)
             store(j)

@@ -21,7 +21,7 @@ P = 128
 PACK = 4
 LIST_COLS = I // 16
 HALF = I // 2
-SCALAR_DEALS = 24
+SCALAR_DEALS = 16
 SCALAR_PLACES = 192
 
 
@@ -63,7 +63,7 @@ def tile_attend_earliertable_deliveredplanes_lean_pl_kernel(
         nc.gpsimd.memset(pool_scales[:].bitcast(I32), 0)
         nc.gpsimd.dma_start(out=row_factor[:], in_=qs.rearrange("(p r) o -> p (r o)", r=PACK))
         for j in range(PACK):
-            (nc.vector if j < 2 else nc.gpsimd).memset(placed[j][:], 0.0)
+            (nc.vector if j < 3 else nc.gpsimd).memset(placed[j][:], 0.0)
 
         earl_by_place = earl.rearrange("(p r) z -> p r z", r=PACK)
         nc.sync.dma_start(out=pool_words[:].bitcast(I32), in_=keys_words[0].bitcast(I32))
@@ -110,7 +110,8 @@ def tile_attend_earliertable_deliveredplanes_lean_pl_kernel(
         earl_listed = [sbuf("earl_listed%d" % r, [P, I], F32, tag="relay" if r == 0 else None) for r in range(PACK)]
         nc.vector.tensor_copy(earl_listed[0][:], earl_rows[0][:].indirect(earl_list[:]))
         nc.scalar.activation(earl_listed[1][:], earl_rows[1][:].indirect(earl_list[:]), COPY)
-        nc.scalar.activation(earl_listed[2][:], earl_rows[2][:].indirect(earl_list[:]), COPY)
+        nc.scalar.activation(earl_listed[2][:, :HALF], earl_rows[2][:].indirect(earl_list[:, : LIST_COLS // 2]), COPY)
+        nc.vector.tensor_copy(earl_listed[2][:, HALF:], earl_rows[2][:].indirect(earl_list[:, LIST_COLS // 2 :]))
         for h in range(2):
             half_list = earl_list[:, h * (LIST_COLS // 2) : (h + 1) * (LIST_COLS // 2)]
             nc.scalar.activation(earl_listed[3][:, h * HALF : (h + 1) * HALF], earl_rows[3][:].indirect(half_list), COPY)

from contextlib import ExitStack

import concourse.mybir as mybir

D, T, I, Q, E, Z, M = 512, 2048, 512, 512, 512, 1024, 1024
FLOPS = 2 * D * Q * I + 2 * Q * E * I

F32 = mybir.dt.float32
BF16 = mybir.dt.bfloat16
I32 = mybir.dt.int32
U32 = mybir.dt.uint32
U16 = mybir.dt.uint16
U8 = mybir.dt.uint8
FP8X4 = mybir.dt.float8_e4m3fn_x4
FP4X4 = mybir.dt.float4_e2m1fn_x4
MULT = mybir.AluOpType.mult
ADD = mybir.AluOpType.add
COPY = mybir.ActivationFunctionType.Copy

P = 128
PACK = 4
LIST_COLS = I // 16
HALF = I // 2
SCALAR_DEALS = 16
SCALAR_PLACES = 192


def dealt_views(grouped, raw):
    dst = grouped.rearrange("p (t m j) -> p m j t", t=PACK, j=PACK)
    src = raw.rearrange("p j (m t) -> p m j t", t=PACK)
    return dst, src


def woven_views(grouped, planes):
    dst = grouped.rearrange("p (c i t) -> p c t i", i=PACK, t=PACK)
    src = planes.rearrange("p t (c i) -> p c t i", i=PACK)
    return dst, src


def tile_attend_earliertable_deliveredplanes_lean_pl_kernel(
    tc, query, keys_words, keys_scales, earl, qs, msgs, old, offs, offs2, offs3, out_0, out_1, out_2
):
    nc = tc.nc
    with ExitStack() as ctx:
        keep = ctx.enter_context(tc.tile_pool(name="keep", bufs=1))
        psum = ctx.enter_context(tc.psum_pool(name="psum", bufs=1))

        def sbuf(name, shape, dtype, tag=None):
            return keep.tile(shape, dtype, name=name, tag=tag or name, align_bytes=64)

        key_list = sbuf("key_list", [P, LIST_COLS], U16)
        earl_list = sbuf("earl_list", [P, LIST_COLS], U16)
        place_list = sbuf("place_list", [P, LIST_COLS], U16)
        query_raw = sbuf("query_raw", [P, PACK, Q], F32)
        pool_words = sbuf("pool_words", [P, T], U16)
        pool_scales = sbuf("pool_scales", [P, T], U8)
        earl_rows = [sbuf("earl_rows%d" % r, [P, Z], F32) for r in range(PACK)]
        row_factor = sbuf("row_factor", [P, PACK], F32)
        msgs_raw = [sbuf("msgs_raw%d" % h, [P, PACK, E // 2], F32) for h in range(2)]
        old_rows = [sbuf("old_rows%d" % h, [P, 2, M], F32) for h in range(2)]
        placed = [sbuf("placed%d" % j, [P, M], F32) for j in range(PACK)]

        nc.gpsimd.memset(pool_scales[:].bitcast(I32), 0)
        nc.gpsimd.dma_start(out=row_factor[:], in_=qs.rearrange("(p r) o -> p (r o)", r=PACK))
        for j in range(PACK):
            (nc.vector if j < 3 else nc.gpsimd).memset(placed[j][:], 0.0)

        earl_by_place = earl.rearrange("(p r) z -> p r z", r=PACK)
        nc.sync.dma_start(out=pool_words[:].bitcast(I32), in_=keys_words[0].bitcast(I32))
        nc.sync.dma_start(key_list[:], offs)
        for quad in range(4):
            nc.sync.dma_start(
                out=pool_scales[32 * quad : 32 * quad + 4, :].bitcast(I32),
                in_=keys_scales[0, 4 * quad : 4 * quad + 4, :].bitcast(I32),
            )
        nc.sync.dma_start(out=query_raw[:], in_=query.rearrange("(p j) q -> p j q", j=PACK))
        for r in range(PACK):
            nc.sync.dma_start(out=earl_rows[r][:], in_=earl_by_place[:, r, :])
            if r == 0:
                nc.sync.dma_start(earl_list[:], offs2)
        msgs_by_place = msgs.rearrange("(p j) e -> p j e", j=PACK)
        for h in range(2):
            nc.sync.dma_start(out=msgs_raw[h][:], in_=msgs_by_place[:, :, h * (E // 2) : (h + 1) * (E // 2)])
        nc.sync.dma_start(place_list[:], offs3)
        old_by_place = old.rearrange("(p j) m -> p j m", j=PACK)
        for h in range(2):
            nc.sync.dma_start(out=old_rows[h][:], in_=old_by_place[:, 2 * h : 2 * h + 2, :])

        query_grouped = [
            sbuf("query_grouped0", [P, 2 * Q], BF16),
            sbuf("query_grouped1", [P, 2 * Q], BF16, tag="relay"),
        ]
        query_codes = sbuf("query_codes", [P, Q], U32)
        query_scales = sbuf("query_scales", [P, Q], U8)
        key_words = sbuf("key_words", [P, I], U16)
        key_scales = sbuf("key_scales", [P, I], U8)
        nc.vector.tensor_copy(key_words[:], pool_words[:].indirect(key_list[:]))
        nc.vector.tensor_copy(key_scales[:], pool_scales[:].indirect(key_list[:]))
        src = query_raw[:].rearrange("p j (m t) -> p m j t", t=PACK)
        for h, copy in enumerate((nc.vector.tensor_copy, nc.scalar.copy)):
            dst = query_grouped[h][:].rearrange("p (t m j) -> p m j t", t=2, j=PACK)
            copy(out=dst, in_=src[:, :, :, 2 * h : 2 * h + 2])
        for h in range(2):
            cols = slice(h * (Q // 2), (h + 1) * (Q // 2))
            nc.vector.quantize_mx(
                out=query_codes[:, cols].bitcast(FP8X4), scales=query_scales[:, cols], in_=query_grouped[h][:]
            )

        weights = sbuf("weights", [P, 2, PACK, HALF], BF16)
        earl_listed = [sbuf("earl_listed%d" % r, [P, I], F32, tag="relay" if r == 0 else None) for r in range(PACK)]
        nc.vector.tensor_copy(earl_listed[0][:], earl_rows[0][:].indirect(earl_list[:]))
        nc.scalar.activation(earl_listed[1][:], earl_rows[1][:].indirect(earl_list[:]), COPY)
        nc.scalar.activation(earl_listed[2][:, :HALF], earl_rows[2][:].indirect(earl_list[:, : LIST_COLS // 2]), COPY)
        nc.vector.tensor_copy(earl_listed[2][:, HALF:], earl_rows[2][:].indirect(earl_list[:, LIST_COLS // 2 :]))
        for h in range(2):
            half_list = earl_list[:, h * (LIST_COLS // 2) : (h + 1) * (LIST_COLS // 2)]
            nc.scalar.activation(earl_listed[3][:, h * HALF : (h + 1) * HALF], earl_rows[3][:].indirect(half_list), COPY)
        for r in range(PACK):
            cols = slice(r * P, (r + 1) * P)
            scores = psum.tile([P, I], F32, name="scores%d" % r)
            nc.tensor.matmul_mx(
                out=scores[:],
                lhsT=query_codes[:, cols].bitcast(FP8X4),
                lhsT_scale=query_scales[:, cols],
                rhs=key_words[:].bitcast(FP4X4),
                rhs_scale=key_scales[:],
                start=True,
                stop=True,
            )
            for halves in (slice(0, 2),) if r < PACK - 1 else (slice(0, 1), slice(1, 2)):
                nc.vector.scalar_tensor_tensor(
                    out=weights[:, halves, r, :],
                    in0=scores[:].rearrange("p (h i) -> p h i", h=2)[:, halves],
                    scalar=row_factor[:, r : r + 1],
                    in1=earl_listed[r][:].rearrange("p (h i) -> p h i", h=2)[:, halves],
                    op0=MULT,
                    op1=MULT,
                )

        grouped = sbuf("grouped", [P, PACK * (HALF + E)], BF16)
        codes = sbuf("codes", [P, HALF + E // 2], U32)
        scales = sbuf("scales", [P, HALF + E // 2], U8)
        late_msgs_codes = sbuf("late_msgs_codes", [P, E // 2], U32)
        late_msgs_scales = sbuf("late_msgs_scales", [P, E // 2], U8)
        late_grouped = sbuf("late_grouped", [P, PACK * HALF], BF16, tag="msgs_raw1")
        late_codes = sbuf("late_codes", [P, HALF], U32)
        late_scales = sbuf("late_scales", [P, HALF], U8)

        def deal_msgs(copy, h, first, last):
            dst, src = dealt_views(grouped[:, PACK * HALF :], msgs_raw[h][:])
            copy(out=dst[:, h * (P // 2) + first : h * (P // 2) + last], in_=src[:, first:last])

        deal_msgs(nc.scalar.copy, 0, 0, P // 2)
        deal_msgs(nc.scalar.copy, 1, 0, SCALAR_DEALS)
        dst, src = woven_views(grouped[:, : PACK * HALF], weights[:, 0])
        nc.vector.tensor_copy(out=dst, in_=src)
        deal_msgs(nc.vector.tensor_copy, 1, SCALAR_DEALS, P // 2)
        split = PACK * (HALF + E // 2)
        nc.vector.quantize_mx(out=codes[:].bitcast(FP8X4), scales=scales[:], in_=grouped[:, :split])
        nc.vector.quantize_mx(out=late_msgs_codes[:].bitcast(FP8X4), scales=late_msgs_scales[:], in_=grouped[:, split:])
        dst, src = woven_views(late_grouped[:], weights[:, 1])
        nc.scalar.copy(out=dst, in_=src)
        nc.vector.quantize_mx(out=late_codes[:].bitcast(FP8X4), scales=late_scales[:], in_=late_grouped[:])

        msgs_operand = [
            (codes[:, HALF + j * P : HALF + (j + 1) * P], scales[:, HALF + j * P : HALF + (j + 1) * P]) for j in range(2)
        ] + [(late_msgs_codes[:, j * P : (j + 1) * P], late_msgs_scales[:, j * P : (j + 1) * P]) for j in range(2)]
        weights_operand = [(codes[:, :HALF], scales[:, :HALF]), (late_codes[:], late_scales[:])]
        banks = {}
        for h in range(2):
            for j in (1, 0, 2, 3) if h == 0 else range(PACK):
                tag = "sums%d" % j if h == 0 else "scores%d" % j
                banks[j, h] = psum.tile([P, HALF], F32, name="sums%d_%d" % (j, h), tag=tag)
                nc.tensor.matmul_mx(
                    out=banks[j, h][:],
                    lhsT=msgs_operand[j][0].bitcast(FP8X4),
                    lhsT_scale=msgs_operand[j][1],
                    rhs=weights_operand[h][0].bitcast(FP8X4),
                    rhs_scale=weights_operand[h][1],
                    start=True,
                    stop=True,
                )

        out_by_place = out_0.rearrange("(p j) m -> p j m", j=PACK)
        result = sbuf("result", [P, PACK, M], F32)

        sums = [sbuf("sums_sb%d" % j, [P, I], F32) for j in range(PACK)]

        def place(on_vector, j, h, first, last):
            out_of_bank = sums[j][:, h * HALF : (h + 1) * HALF]
            window = placed[j][:].indirect(place_list[:, first // 16 : last // 16])
            if on_vector:
                nc.vector.tensor_copy(out=out_of_bank, in_=banks[j, h][:])
                nc.vector.tensor_copy(window, sums[j][:, first:last])
            else:
                nc.scalar.copy(out=out_of_bank, in_=banks[j, h][:])
                nc.scalar.activation(window, sums[j][:, first:last], COPY)

        def add_old(j, first, last):
            nc.vector.tensor_tensor(
                out=result[:, j, first:last], in0=old_rows[j // 2][:, j % 2, first:last], in1=placed[j][:, first:last], op=ADD
            )

        def store(j):
            nc.sync.dma_start(out=out_by_place[:, j, :], in_=result[:, j, :])

        place(False, 1, 0, 0, SCALAR_PLACES)
        for j in (2, 3):
            for h in range(2):
                place(False, j, h, h * HALF, (h + 1) * HALF)
        for h in range(2):
            place(True, 0, h, h * HALF, (h + 1) * HALF)
        place(True, 1, 1, SCALAR_PLACES, I)
        for j in (0, 1, 2):
            add_old(j, 0, M)
            store(j)
        pieces = ((0, 256), (256, 512), (512, M))
        for first, last in (pieces[0], pieces[2], pieces[1]):
            add_old(3, first, last)
        store(3)

        result_grouped = sbuf("result_grouped", [P, PACK * M], BF16)
        result_codes = sbuf("result_codes", [P, M], U32)
        result_scales = sbuf("result_scales", [P, M], U8)
        dst, src = woven_views(result_grouped[:], result[:])
        out_words = out_1[0].rearrange("p c r -> p (c r)").bitcast(I32)
        for (first, last), copy in zip(pieces, (nc.scalar.copy, nc.scalar.copy, nc.vector.tensor_copy)):
            copy(out=dst[:, first // PACK : last // PACK], in_=src[:, first // PACK : last // PACK])
        for first, last in (pieces[0], pieces[2], pieces[1]):
            nc.vector.quantize_mx(
                out=result_codes[:, first:last].bitcast(FP8X4),
                scales=result_scales[:, first:last],
                in_=result_grouped[:, first * PACK : last * PACK],
            )
            nc.sync.dma_start(out=out_words[:, first:last], in_=result_codes[:, first:last].bitcast(I32))
        for quad in range(4):
            queue = nc.scalar if quad % 2 == 0 else nc.sync
            queue.dma_start(
                out=out_2[0, 4 * quad : 4 * quad + 4, :].bitcast(I32),
                in_=result_scales[32 * quad : 32 * quad + 4, :].bitcast(I32),
            )
